import numpy as np, ml_dtypes
CORES = [21,85,149,213,277,341,405,469]
N = 8
import mx_ref
NC, G = 128, 2
C = np.float32(0.031)
BF = ml_dtypes.bfloat16
def tile(rs):
    return np.stack(rs, axis=2).reshape(128, -1).astype(BF)
def act(Z):
    return [np.maximum(s * z, 0) * C for z in Z for s in (1, -1)]
def pk(c, s, i=0):
    return (np.ascontiguousarray(c[:, 512 * i:512 * i + 512]), mx_ref.live(s[:, 128 * i:128 * i + 128]))
def inputs(rng, e, E):
    def f(*shape):
        v = (rng.standard_normal(shape, dtype=np.float32) * np.exp2(rng.integers(-2, 3, shape[:-1] + (1,)))).astype(BF)
        return mx_ref.spread((v.astype(np.float32) * np.exp2(rng.integers(-E, E + 1, shape[:-2] + (1, 1))).astype(np.float32)).astype(BF), rng, e)
    def packed(k):
        c = np.zeros((N, 128, k * 512), np.uint8); s = np.zeros((N, 128, k * 128), np.uint8)
        for r in range(N):
            for i in range(k):
                a, b = mx_ref.quantize(f(128, 512)); c[r][:, 512 * i:512 * i + 512] = a; s[r][:, 128 * i:128 * i + 128] = mx_ref.plane(b, rng)
        return c, s
    d = {}
    d["ac"], d["az"] = packed(1)
    d["bc"], d["bs"] = packed(1)
    d["x"] = f(N, 128, 4 * NC)
    return d
def setup_inputs(rng):
    return inputs(rng, 0, 0)
def setup_inputs_blocks(rng):
    return inputs(rng, 4, 0)
def setup_inputs_wide(rng):
    return inputs(rng, 0, 8)
def reference(ac, az, bc, bs, x):
    y = np.zeros((N, 128, N * NC), np.float32)
    for r in range(N):
        X = mx_ref.quantize(x[r])
        h = mx_ref.quantize(tile(act([mx_ref.matmul(pk(ac[i], az[i]), X) for i in range(G)])))
        for j in range(N):
            y[r][:, NC * j:NC * j + NC] = mx_ref.matmul(pk(bc[j], bs[j]), h)
    return {"y": y}

@@ -1,0 +1,177 @@
+from concourse.bass import DstId, RemoteDMATransfer
+from concourse.mybir import dt, AluOpType, ActivationFunctionType
+
+N, NC, G = 8, 128, 2
+C = 0.031
+SLOT_B = [0, 3] + [j + 2 for j in range(2, N)]
+SLOT_A = [1, 2]
+NSLOT = N + G
+
+SCRATCH = {
+    "wc": ("sbuf", [128, NSLOT * NC], "float8_e4m3fn_x4"),
+    "ws": ("sbuf", [128, NSLOT * NC], "uint8"),
+    "xt": ("sbuf", [128, 4 * NC], "bfloat16"),
+    "xq": ("sbuf", [128, NC], "float8_e4m3fn_x4"),
+    "xs": ("sbuf", [128, NC], "uint8"),
+    "ht": ("sbuf", [128, 4 * NC], "bfloat16"),
+    "hq": ("sbuf", [128, NC], "float8_e4m3fn_x4"),
+    "hs": ("sbuf", [128, NC], "uint8"),
+    "yt": ("sbuf", [128, N * NC], "float32"),
+    "ps": ("psum", [128, 8 * 512], "float32"),
+}
+SEMAPHORES = (["lp", "lc", "lx", "sent", "xr", "z0", "z1", "hr", "hd", "st"]
+              + ["a%d" % s for s in range(NSLOT)] + ["m%d" % k for k in range(N)] + ["c%d" % k for k in range(N)])
+
+
+def _own(r):
+    s = [SLOT_B[r]] + ([SLOT_A[r]] if r < G else [])
+    return min(s), max(s) + 1
+
+
+def _plan(cores, topo):
+    n = len(cores)
+
+    def ok(a, b):
+        return topo.may_write(cores[a], cores[b])
+
+    direct = [[d for d in range(n) if d != r and ok(r, d)] for r in range(n)]
+    far = [[s for s in range(n) if s != d and not ok(s, d)] for d in range(n)]
+    frun = [(min(_own(s)[0] for s in far[d]), max(_own(s)[1] for s in far[d])) for d in range(n)]
+    load = [(_own(r)[1] - _own(r)[0]) * len(direct[r]) for r in range(n)]
+    relay = {}
+    for d in sorted(range(n), key=lambda d: (frun[d][0] - frun[d][1], d)):
+        cand = [q for q in range(n) if q != d and ok(q, d) and all(ok(s, q) for s in far[d])
+                and topo.chip(cores[q]) == topo.chip(cores[d])]
+        q = min(cand, key=lambda q: (load[q], topo.same_plane(cores[q], cores[d]), q))
+        relay[d] = q
+        load[q] += frun[d][1] - frun[d][0]
+    sends, got = [], [dict() for _ in range(n)]
+    for r in range(n):
+        first = sorted({relay[d] for d in range(n) if r in far[d]})
+        rest = [d for d in direct[r] if d not in first]
+        rest = sorted(rest, key=lambda d: (d - r) % n)
+        sends.append([(_own(r), first), (_own(r), rest)] + [(frun[d], [d]) for d in range(n) if relay[d] == r])
+        for s in range(*_own(r)):
+            got[r][s] = (None, 0)
+        for k, (run, ds) in enumerate(sends[r]):
+            for d in ds:
+                for s in range(*run):
+                    got[d][s] = (run[0], min(k, 2) + 1)
+    return sends, got
+
+
+def rank_program(g, core, T, topo):
+    rank = T.rank_of(core)
+    if rank is None:
+        return
+    cores = list(T.cores)
+    sends, got = _plan(cores, topo)
+    S = T.sem
+    mine = got[rank]
+
+    def codes(lo, hi):
+        return T.wc[:, lo * NC:hi * NC].bitcast(dt.uint8)
+
+    def plane(lo, hi):
+        return T.ws[:, lo * NC:hi * NC]
+
+    nl = 0
+    if rank < G:
+        a = SLOT_A[rank]
+        g.scalar.dma_start(plane(a, a + 1), T.az[:, :]).then_inc(S.lp, 16)
+        g.sync.dma_start(codes(a, a + 1), T.ac[:, :]).then_inc(S.lc, 16)
+        nl += 16
+    b = SLOT_B[rank]
+    g.scalar.dma_start(plane(b, b + 1), T.bs[:, :]).then_inc(S.lp, 16)
+    g.sync.dma_start(codes(b, b + 1), T.bc[:, :]).then_inc(S.lc, 16)
+    nl += 16
+    g.scalar.dma_start(T.xt[:, :], T.x[:, :]).then_inc(S.lx, 16)
+
+    nsent = 0
+    waited = set()
+    need = {}
+    for r in range(len(cores)):
+        for run, ds in sends[r]:
+            if rank in ds:
+                m = topo.mask(cores[r], core)
+                for d in ds:
+                    m &= topo.mask(cores[r], cores[d])
+                need[run[0]] = 2 * bin(m).count("1")
+
+    def await_slot(q, s, part):
+        lo = mine[s][0]
+        if lo is None:
+            if part in ("p", "b"):
+                q.wait_ge(S.lp, nl)
+            if part in ("c", "b"):
+                q.wait_ge(S.lc, nl)
+        else:
+            q.wait_ge(S["a%d" % lo], need[lo])
+
+    for run, ds in sends[rank]:
+        if not ds:
+            continue
+        m = -1
+        for d in ds:
+            m &= topo.mask(core, cores[d])
+        ne = bin(m).count("1")
+        ids = []
+        for d in ds:
+            rid, pid = topo.addr(cores[d], core)
+            ids.append(DstId(rid=rid, pnc=pid))
+        for part, view in (("p", plane), ("c", codes)):
+            for s in range(*run):
+                key = (mine[s][0], part if mine[s][0] is None else "b")
+                if key not in waited:
+                    waited.add(key)
+                    await_slot(g, s, part)
+            g.remote_dma_fused(
+                [RemoteDMATransfer(dst_ids=ids, dma_engine_mask=m, remote_sem=S["a%d" % run[0]],
+                                   srcs=[view(*run)], dsts=[view(*run) for _ in ds])],
+                local_sem=S.sent)
+            nsent += ne
+    g.wait_ge(S.sent, nsent)
+
+    v, sc, te = g.vector, g.scalar, g.tensor
+    v.wait_ge(S.lx, 16)
+    v.quantize_mx(T.xq[:, :], T.xs[:, :], T.xt[:, :]).then_inc(S.xr, 1)
+    te.wait_ge(S.xr, 1)
+    for i in range(G):
+        a = SLOT_A[i]
+        await_slot(te, a, "b")
+        te.matmul_mx(T.ps[:, 512 * i:512 * i + NC], T.wc[:, a * NC:(a + 1) * NC], T.ws[:, a * NC:(a + 1) * NC],
+                     T.xq[:, :], T.xs[:, :], True, True).then_inc(S["z%d" % i], 1)
+    v.wait_ge(S.z0, 1)
+    v.tensor_scalar(out=T.ht[:, 0:4 * NC:4], in0=T.ps[:, 0:NC], scalar1=0.0, scalar2=C,
+                    op0=AluOpType.max, op1=AluOpType.mult).then_inc(S.hr, 1)
+    v.tensor_scalar(out=T.ht[:, 1:4 * NC:4], in0=T.ps[:, 0:NC], scalar1=-C, scalar2=0.0,
+                    op0=AluOpType.mult, op1=AluOpType.max).then_inc(S.hr, 1)
+    sc.wait_ge(S.z1, 1)
+    sc.activation(T.ht[:, 2:4 * NC:4], T.ps[:, 512:512 + NC], ActivationFunctionType.Relu, scale=C).then_inc(S.hr, 1)
+    sc.activation(T.ht[:, 3:4 * NC:4], T.ps[:, 512:512 + NC], ActivationFunctionType.Relu, scale=-C).then_inc(S.hr, 1)
+    v.wait_ge(S.hr, 4)
+    v.quantize_mx(T.hq[:, :], T.hs[:, :], T.ht[:, :]).then_inc(S.hd, 1)
+    te.wait_ge(S.hd, 1)
+
+    pairs = [[j for j in range(N) if topo.host(cores[j]) == h] for h in sorted({topo.host(c) for c in cores})]
+    pairs.sort(key=lambda p: (max(mine[SLOT_B[j]][1] for j in p), p[0]))
+    k = 0
+    for gi, p in enumerate(pairs):
+        for j in sorted(p, key=lambda j: mine[SLOT_B[j]][1]):
+            s = SLOT_B[j]
+            bank = (G + k) % 8
+            out = T.ps[:, 512 * bank:512 * bank + NC]
+            await_slot(te, s, "b")
+            te.matmul_mx(out, T.wc[:, s * NC:(s + 1) * NC], T.ws[:, s * NC:(s + 1) * NC],
+                         T.hq[:, :], T.hs[:, :], True, True).then_inc(S["m%d" % k], 1)
+            if k % 2 == 0:
+                v.wait_ge(S["m%d" % k], 1)
+                v.tensor_copy(T.yt[:, j * NC:(j + 1) * NC], out).then_inc(S["c%d" % gi], 1)
+            else:
+                sc.wait_ge(S["m%d" % k], 1)
+                sc.activation(T.yt[:, j * NC:(j + 1) * NC], out, ActivationFunctionType.Copy).then_inc(S["c%d" % gi], 1)
+            k += 1
+        lo, hi = min(p) * NC, (max(p) + 1) * NC
+        g.sync.wait_ge(S["c%d" % gi], len(p))
+        g.sync.dma_start(T.y[:, lo:hi], T.yt[:, lo:hi]).then_inc(S.st, 16)
+    g.sync.wait_ge(S.st, 16 * len(pairs))

@@ -23,41 +23,83 @@ SEMAPHORES = (["lp", "lc", "lx", "sent", "xr", "z0", "z1", "hr", "hd", "st"]
               + ["a%d" % s for s in range(NSLOT)] + ["m%d" % k for k in range(N)] + ["c%d" % k for k in range(N)])
 
 
-def _own(r):
-    s = [SLOT_B[r]] + ([SLOT_A[r]] if r < G else [])
-    return min(s), max(s) + 1
+def _part(m, kind):
+    bits = [b for b in range(32) if (m >> b) & 1]
+    if kind == "c":
+        bits = bits[1::2]
+    elif kind == "s":
+        bits = bits[0::2]
+    out = 0
+    for b in bits:
+        out |= 1 << b
+    return out
 
 
 def _plan(cores, topo):
     n = len(cores)
+    lam = 1.0
 
     def ok(a, b):
         return topo.may_write(cores[a], cores[b])
 
-    direct = [[d for d in range(n) if d != r and ok(r, d)] for r in range(n)]
-    far = [[s for s in range(n) if s != d and not ok(s, d)] for d in range(n)]
-    frun = [(min(_own(s)[0] for s in far[d]), max(_own(s)[1] for s in far[d])) for d in range(n)]
-    load = [(_own(r)[1] - _own(r)[0]) * len(direct[r]) for r in range(n)]
-    relay = {}
-    for d in sorted(range(n), key=lambda d: (frun[d][0] - frun[d][1], d)):
-        cand = [q for q in range(n) if q != d and ok(q, d) and all(ok(s, q) for s in far[d])
-                and topo.chip(cores[q]) == topo.chip(cores[d])]
-        q = min(cand, key=lambda q: (load[q], topo.same_plane(cores[q], cores[d]), q))
-        relay[d] = q
-        load[q] += frun[d][1] - frun[d][0]
-    sends, got = [], [dict() for _ in range(n)]
+    def rk(r):
+        return topo.rack(topo.host(cores[r]))
+
+    def same_host(a, b):
+        return topo.host(cores[a]) == topo.host(cores[b])
+
+    def same_no(a, b):
+        return topo.chip(cores[a]) == topo.chip(cores[b])
+
+    mates = [[q for q in range(n) if topo.same_plane(cores[r], cores[q])] for r in range(n)]
+    part = [[q for q in range(n) if rk(q) != rk(r) and ok(r, q) and same_no(r, q)][0] for r in range(n)]
+    order = [sorted(mates[r], key=lambda q: (same_host(r, q), not same_no(r, q))) for r in range(n)]
+    owner = {}
+    for j in range(N):
+        owner[SLOT_B[j]] = j
+    for i in range(G):
+        owner[SLOT_A[i]] = i
+    owned = [SLOT_A[r:r + 1] + [SLOT_B[r]] for r in range(n)]
+    calls = [[] for _ in range(n)]
+    est = [dict() for _ in range(n)]
+    tq = [{"c": 0.0, "s": 0.0} for _ in range(n)]
+
+    def book(r, s, ds, kind, ready):
+        t = max(tq[r][kind], ready)
+        for d in ds:
+            t += 1.0
+            est[d][s] = t + lam
+        tq[r][kind] = t
+
     for r in range(n):
-        first = sorted({relay[d] for d in range(n) if r in far[d]})
-        rest = [d for d in direct[r] if d not in first]
-        rest = sorted(rest, key=lambda d: (d - r) % n)
-        sends.append([(_own(r), first), (_own(r), rest)] + [(frun[d], [d]) for d in range(n) if relay[d] == r])
-        for s in range(*_own(r)):
-            got[r][s] = (None, 0)
-        for k, (run, ds) in enumerate(sends[r]):
-            for d in ds:
-                for s in range(*run):
-                    got[d][s] = (run[0], min(k, 2) + 1)
-    return sends, got
+        for k, s in enumerate(owned[r]):
+            est[r][s] = 0.0
+            ds = order[r] if k == 0 else order[r][-1:] + order[r][:-1]
+            calls[r].append([(s, s + 1, [part[r]], "c"), (s, s + 1, ds, "s")])
+            book(r, s, [part[r]], "c", 0.0)
+            book(r, s, ds, "s", 0.0)
+    cf = [[] for _ in range(n)]
+    sf = [dict() for _ in range(n)]
+    for d in range(n):
+        cin = len(owned[part[d]])
+        sin = sum(len(owned[q]) for q in mates[d])
+        todo = [s for s in SLOT_A + SLOT_B if rk(owner[s]) != rk(d) and owner[s] != part[d]]
+        for s in sorted(todo, key=lambda s: (s not in SLOT_A, not ok(owner[s], d), owner[s])):
+            o = owner[s]
+            if s in SLOT_A or cin < sin or (cin == sin and ok(o, d)):
+                cin += 1
+                cf[part[d]].append(s)
+            else:
+                sin += 1
+                sf[part[o]].setdefault(s, []).append(d)
+    for r in range(n):
+        items = [(est[r][s], 0, s, [part[r]], "c") for s in cf[r]]
+        items += [(est[r][s], 1, s, [q for q in order[r] if q in sf[r][s]], "s") for s in sf[r]]
+        for ready, _, s, ds, kind in sorted(items):
+            calls[r].append([(s, s + 1, ds, kind)])
+            book(r, s, ds, kind, ready)
+    got = [{s: (None if owner[s] == d else s, est[d][s]) for s in est[d]} for d in range(n)]
+    return calls, got
 
 
 def rank_program(g, core, T, topo):
@@ -65,7 +107,7 @@ def rank_program(g, core, T, topo):
     if rank is None:
         return
     cores = list(T.cores)
-    sends, got = _plan(cores, topo)
+    calls, got = _plan(cores, topo)
     S = T.sem
     mine = got[rank]
 
@@ -74,6 +116,12 @@ def rank_program(g, core, T, topo):
 
     def plane(lo, hi):
         return T.ws[:, lo * NC:hi * NC]
+
+    def engines(src, ds, kind):
+        m = -1
+        for d in ds:
+            m &= topo.mask(cores[src], cores[d])
+        return _part(m, kind)
 
     nl = 0
     if rank < G:
@@ -87,16 +135,12 @@ def rank_program(g, core, T, topo):
     nl += 16
     g.scalar.dma_start(T.xt[:, :], T.x[:, :]).then_inc(S.lx, 16)
 
-    nsent = 0
-    waited = set()
     need = {}
     for r in range(len(cores)):
-        for run, ds in sends[r]:
-            if rank in ds:
-                m = topo.mask(cores[r], core)
-                for d in ds:
-                    m &= topo.mask(cores[r], cores[d])
-                need[run[0]] = 2 * bin(m).count("1")
+        for call in calls[r]:
+            for lo, hi, ds, kind in call:
+                if rank in ds:
+                    need[lo] = 2 * bin(engines(r, ds, kind)).count("1")
 
     def await_slot(q, s, part):
         lo = mine[s][0]
@@ -108,35 +152,33 @@ def rank_program(g, core, T, topo):
         else:
             q.wait_ge(S["a%d" % lo], need[lo])
 
-    for run, ds in sends[rank]:
-        if not ds:
-            continue
-        m = -1
-        for d in ds:
-            m &= topo.mask(core, cores[d])
-        ne = bin(m).count("1")
-        ids = []
-        for d in ds:
-            rid, pid = topo.addr(cores[d], core)
-            ids.append(DstId(rid=rid, pnc=pid))
+    nsent = 0
+    waited = set()
+    for call in calls[rank]:
         for part, view in (("p", plane), ("c", codes)):
-            for s in range(*run):
-                key = (mine[s][0], part if mine[s][0] is None else "b")
-                if key not in waited:
-                    waited.add(key)
-                    await_slot(g, s, part)
-            g.remote_dma_fused(
-                [RemoteDMATransfer(dst_ids=ids, dma_engine_mask=m, remote_sem=S["a%d" % run[0]],
-                                   srcs=[view(*run)], dsts=[view(*run) for _ in ds])],
-                local_sem=S.sent)
-            nsent += ne
+            trs = []
+            for lo, hi, ds, kind in call:
+                for s in range(lo, hi):
+                    key = (mine[s][0], part if mine[s][0] is None else "b")
+                    if key not in waited:
+                        waited.add(key)
+                        await_slot(g, s, part)
+                m = engines(rank, ds, kind)
+                ids = []
+                for d in ds:
+                    rid, pid = topo.addr(cores[d], core)
+                    ids.append(DstId(rid=rid, pnc=pid))
+                trs.append(RemoteDMATransfer(dst_ids=ids, dma_engine_mask=m, remote_sem=S["a%d" % lo],
+                                             srcs=[view(lo, hi)], dsts=[view(lo, hi) for _ in ds]))
+                nsent += bin(m).count("1")
+            g.remote_dma_fused(trs, local_sem=S.sent)
     g.wait_ge(S.sent, nsent)
 
     v, sc, te = g.vector, g.scalar, g.tensor
     v.wait_ge(S.lx, 16)
     v.quantize_mx(T.xq[:, :], T.xs[:, :], T.xt[:, :]).then_inc(S.xr, 1)
     te.wait_ge(S.xr, 1)
-    for i in range(G):
+    for i in sorted(range(G), key=lambda i: mine[SLOT_A[i]][1]):
         a = SLOT_A[i]
         await_slot(te, a, "b")
         te.matmul_mx(T.ps[:, 512 * i:512 * i + NC], T.wc[:, a * NC:(a + 1) * NC], T.ws[:, a * NC:(a + 1) * NC],

@@ -19,16 +19,14 @@ SCRATCH = {
     "yt": ("sbuf", [128, N * NC], "float32"),
     "ps": ("psum", [128, 8 * 512], "float32"),
 }
-SEMAPHORES = (["lp", "lc", "lx", "sent", "xr", "z0", "z1", "hr", "hd", "st"]
-              + ["a%d" % s for s in range(NSLOT)] + ["m%d" % k for k in range(N)] + ["c%d" % k for k in range(N)])
+SEMAPHORES = (["lx", "sent", "xr", "z0", "z1", "hr", "hd", "st"]
+              + ["p%d" % s for s in range(NSLOT)] + ["q%d" % s for s in range(NSLOT)]
+              + ["m%d" % k for k in range(N)] + ["c%d" % k for k in range(N)])
 
 
 def _part(m, kind):
     bits = [b for b in range(32) if (m >> b) & 1]
-    if kind == "c":
-        bits = bits[1::2]
-    elif kind == "s":
-        bits = bits[0::2]
+    bits = bits[1::2] if kind == "c" else bits[0::2]
     out = 0
     for b in bits:
         out |= 1 << b
@@ -75,30 +73,30 @@ def _plan(cores, topo):
         for k, s in enumerate(owned[r]):
             est[r][s] = 0.0
             ds = order[r] if k == 0 else order[r][-1:] + order[r][:-1]
-            calls[r].append([(s, s + 1, [part[r]], "c"), (s, s + 1, ds, "s")])
+            if k == 0:
+                calls[r].append([(s, ds, "s")])
+                calls[r].append([(s, [part[r]], "c")])
+            else:
+                calls[r].append([(s, [part[r]], "c"), (s, ds, "s")])
             book(r, s, [part[r]], "c", 0.0)
             book(r, s, ds, "s", 0.0)
     cf = [[] for _ in range(n)]
     sf = [dict() for _ in range(n)]
     for d in range(n):
-        cin = len(owned[part[d]])
-        sin = sum(len(owned[q]) for q in mates[d])
         todo = [s for s in SLOT_A + SLOT_B if rk(owner[s]) != rk(d) and owner[s] != part[d]]
         for s in sorted(todo, key=lambda s: (s not in SLOT_A, not ok(owner[s], d), owner[s])):
             o = owner[s]
-            if s in SLOT_A or cin < sin or (cin == sin and ok(o, d)):
-                cin += 1
+            if s in SLOT_A or len(owned[part[o]]) > 1:
                 cf[part[d]].append(s)
             else:
-                sin += 1
                 sf[part[o]].setdefault(s, []).append(d)
     for r in range(n):
         items = [(est[r][s], 0, s, [part[r]], "c") for s in cf[r]]
         items += [(est[r][s], 1, s, [q for q in order[r] if q in sf[r][s]], "s") for s in sf[r]]
         for ready, _, s, ds, kind in sorted(items):
-            calls[r].append([(s, s + 1, ds, kind)])
+            calls[r].append([(s, ds, kind)])
             book(r, s, ds, kind, ready)
-    got = [{s: (None if owner[s] == d else s, est[d][s]) for s in est[d]} for d in range(n)]
+    got = [{s: (owner[s] == d, est[d][s]) for s in est[d]} for d in range(n)]
     return calls, got
 
 
@@ -111,11 +109,11 @@ def rank_program(g, core, T, topo):
     S = T.sem
     mine = got[rank]
 
-    def codes(lo, hi):
-        return T.wc[:, lo * NC:hi * NC].bitcast(dt.uint8)
+    def codes(s):
+        return T.wc[:, s * NC:(s + 1) * NC].bitcast(dt.uint8)
 
-    def plane(lo, hi):
-        return T.ws[:, lo * NC:hi * NC]
+    def plane(s):
+        return T.ws[:, s * NC:(s + 1) * NC]
 
     def engines(src, ds, kind):
         m = -1
@@ -123,53 +121,42 @@ def rank_program(g, core, T, topo):
             m &= topo.mask(cores[src], cores[d])
         return _part(m, kind)
 
-    nl = 0
     if rank < G:
         a = SLOT_A[rank]
-        g.scalar.dma_start(plane(a, a + 1), T.az[:, :]).then_inc(S.lp, 16)
-        g.sync.dma_start(codes(a, a + 1), T.ac[:, :]).then_inc(S.lc, 16)
-        nl += 16
+        g.scalar.dma_start(plane(a), T.az[:, :]).then_inc(S["p%d" % a], 16)
+        g.sync.dma_start(codes(a), T.ac[:, :]).then_inc(S["q%d" % a], 16)
     b = SLOT_B[rank]
-    g.scalar.dma_start(plane(b, b + 1), T.bs[:, :]).then_inc(S.lp, 16)
-    g.sync.dma_start(codes(b, b + 1), T.bc[:, :]).then_inc(S.lc, 16)
-    nl += 16
+    g.scalar.dma_start(plane(b), T.bs[:, :]).then_inc(S["p%d" % b], 16)
+    g.sync.dma_start(codes(b), T.bc[:, :]).then_inc(S["q%d" % b], 16)
     g.scalar.dma_start(T.xt[:, :], T.x[:, :]).then_inc(S.lx, 16)
 
-    need = {}
+    need = {s: 16 for s in mine if mine[s][0]}
     for r in range(len(cores)):
         for call in calls[r]:
-            for lo, hi, ds, kind in call:
+            for s, ds, kind in call:
                 if rank in ds:
-                    need[lo] = 2 * bin(engines(r, ds, kind)).count("1")
+                    need[s] = bin(engines(r, ds, kind)).count("1")
 
-    def await_slot(q, s, part):
-        lo = mine[s][0]
-        if lo is None:
-            if part in ("p", "b"):
-                q.wait_ge(S.lp, nl)
-            if part in ("c", "b"):
-                q.wait_ge(S.lc, nl)
-        else:
-            q.wait_ge(S["a%d" % lo], need[lo])
+    def await_slot(q, s, parts):
+        for part in parts:
+            q.wait_ge(S["%s%d" % (part, s)], need[s])
 
     nsent = 0
     waited = set()
     for call in calls[rank]:
-        for part, view in (("p", plane), ("c", codes)):
+        for part, view in (("p", plane), ("q", codes)):
             trs = []
-            for lo, hi, ds, kind in call:
-                for s in range(lo, hi):
-                    key = (mine[s][0], part if mine[s][0] is None else "b")
-                    if key not in waited:
-                        waited.add(key)
-                        await_slot(g, s, part)
+            for s, ds, kind in call:
+                if (s, part) not in waited:
+                    waited.add((s, part))
+                    await_slot(g, s, part)
                 m = engines(rank, ds, kind)
                 ids = []
                 for d in ds:
                     rid, pid = topo.addr(cores[d], core)
                     ids.append(DstId(rid=rid, pnc=pid))
-                trs.append(RemoteDMATransfer(dst_ids=ids, dma_engine_mask=m, remote_sem=S["a%d" % lo],
-                                             srcs=[view(lo, hi)], dsts=[view(lo, hi) for _ in ds]))
+                trs.append(RemoteDMATransfer(dst_ids=ids, dma_engine_mask=m, remote_sem=S["%s%d" % (part, s)],
+                                             srcs=[view(s)], dsts=[view(s) for _ in ds]))
                 nsent += bin(m).count("1")
             g.remote_dma_fused(trs, local_sem=S.sent)
     g.wait_ge(S.sent, nsent)
@@ -180,7 +167,7 @@ def rank_program(g, core, T, topo):
     te.wait_ge(S.xr, 1)
     for i in sorted(range(G), key=lambda i: mine[SLOT_A[i]][1]):
         a = SLOT_A[i]
-        await_slot(te, a, "b")
+        await_slot(te, a, "pq")
         te.matmul_mx(T.ps[:, 512 * i:512 * i + NC], T.wc[:, a * NC:(a + 1) * NC], T.ws[:, a * NC:(a + 1) * NC],
                      T.xq[:, :], T.xs[:, :], True, True).then_inc(S["z%d" % i], 1)
     v.wait_ge(S.z0, 1)
@@ -203,7 +190,7 @@ def rank_program(g, core, T, topo):
             s = SLOT_B[j]
             bank = (G + k) % 8
             out = T.ps[:, 512 * bank:512 * bank + NC]
-            await_slot(te, s, "b")
+            await_slot(te, s, "pq")
             te.matmul_mx(out, T.wc[:, s * NC:(s + 1) * NC], T.ws[:, s * NC:(s + 1) * NC],
                          T.hq[:, :], T.hs[:, :], True, True).then_inc(S["m%d" % k], 1)
             if k % 2 == 0:

@@ -19,8 +19,8 @@ SCRATCH = {
     "yt": ("sbuf", [128, N * NC], "float32"),
     "ps": ("psum", [128, 8 * 512], "float32"),
 }
-SEMAPHORES = (["lx", "sent", "xr", "z0", "z1", "hr", "hd", "st"]
-              + ["p%d" % s for s in range(NSLOT)] + ["q%d" % s for s in range(NSLOT)]
+SEMAPHORES = (["lx", "sent", "xr", "z0", "z1", "hr", "hd", "st", "pl", "pc"]
+              + ["g%d" % r for r in range(N)] + ["q%d" % s for s in range(NSLOT)]
               + ["m%d" % k for k in range(N)] + ["c%d" % k for k in range(N)])
 
 
@@ -97,7 +97,7 @@ def _plan(cores, topo):
             calls[r].append([(s, ds, kind)])
             book(r, s, ds, kind, ready)
     got = [{s: (owner[s] == d, est[d][s]) for s in est[d]} for d in range(n)]
-    return calls, got
+    return calls, got, part, order, owned
 
 
 def rank_program(g, core, T, topo):
@@ -105,15 +105,26 @@ def rank_program(g, core, T, topo):
     if rank is None:
         return
     cores = list(T.cores)
-    calls, got = _plan(cores, topo)
+    calls, got, part, order, owned = _plan(cores, topo)
     S = T.sem
     mine = got[rank]
+
+    pos, span, grp = {}, {}, {}
+    for r in range(len(cores)):
+        if r < part[r]:
+            lo = len(pos)
+            for q in (r, part[r]):
+                a0 = len(pos)
+                for s in owned[q]:
+                    pos[s] = len(pos)
+                span[q] = (a0 * NC, len(pos) * NC)
+            grp[r] = grp[part[r]] = (lo * NC, len(pos) * NC)
 
     def codes(s):
         return T.wc[:, s * NC:(s + 1) * NC].bitcast(dt.uint8)
 
     def plane(s):
-        return T.ws[:, s * NC:(s + 1) * NC]
+        return T.ws[:, pos[s] * NC:(pos[s] + 1) * NC]
 
     def engines(src, ds, kind):
         m = -1
@@ -121,12 +132,23 @@ def rank_program(g, core, T, topo):
             m &= topo.mask(cores[src], cores[d])
         return _part(m, kind)
 
+    def count(src, ds, kind):
+        return bin(engines(src, ds, kind)).count("1")
+
+    def transfer(view, ds, kind, sem):
+        ids = []
+        for d in ds:
+            rid, pid = topo.addr(cores[d], core)
+            ids.append(DstId(rid=rid, pnc=pid))
+        return RemoteDMATransfer(dst_ids=ids, dma_engine_mask=engines(rank, ds, kind), remote_sem=sem,
+                                 srcs=[view], dsts=[view for _ in ds])
+
     if rank < G:
         a = SLOT_A[rank]
-        g.scalar.dma_start(plane(a), T.az[:, :]).then_inc(S["p%d" % a], 16)
+        g.scalar.dma_start(plane(a), T.az[:, :]).then_inc(S.pl, 16)
         g.sync.dma_start(codes(a), T.ac[:, :]).then_inc(S["q%d" % a], 16)
     b = SLOT_B[rank]
-    g.scalar.dma_start(plane(b), T.bs[:, :]).then_inc(S["p%d" % b], 16)
+    g.scalar.dma_start(plane(b), T.bs[:, :]).then_inc(S.pl, 16)
     g.sync.dma_start(codes(b), T.bc[:, :]).then_inc(S["q%d" % b], 16)
     g.scalar.dma_start(T.xt[:, :], T.x[:, :]).then_inc(S.lx, 16)
 
@@ -135,30 +157,43 @@ def rank_program(g, core, T, topo):
         for call in calls[r]:
             for s, ds, kind in call:
                 if rank in ds:
-                    need[s] = bin(engines(r, ds, kind)).count("1")
+                    need[s] = count(r, ds, kind)
+
+    def await_plane(q, s):
+        if s in owned[rank]:
+            q.wait_ge(S.pl, 16 * len(owned[rank]))
+        elif s in owned[part[rank]]:
+            q.wait_ge(S.pc, count(part[rank], [rank], "c"))
+        else:
+            m = [m for m in order[rank] if s in owned[m] or s in owned[part[m]]][0]
+            q.wait_ge(S["g%d" % m], count(m, order[m], "s"))
 
     def await_slot(q, s, parts):
-        for part in parts:
-            q.wait_ge(S["%s%d" % (part, s)], need[s])
+        if "p" in parts:
+            await_plane(q, s)
+        if "q" in parts:
+            q.wait_ge(S["q%d" % s], need[s])
 
     nsent = 0
+    await_plane(g, owned[rank][0])
+    lo, hi = span[rank]
+    g.remote_dma_fused([transfer(T.ws[:, lo:hi], [part[rank]], "c", S.pc)], local_sem=S.sent)
+    nsent += count(rank, [part[rank]], "c")
     waited = set()
-    for call in calls[rank]:
-        for part, view in (("p", plane), ("q", codes)):
-            trs = []
-            for s, ds, kind in call:
-                if (s, part) not in waited:
-                    waited.add((s, part))
-                    await_slot(g, s, part)
-                m = engines(rank, ds, kind)
-                ids = []
-                for d in ds:
-                    rid, pid = topo.addr(cores[d], core)
-                    ids.append(DstId(rid=rid, pnc=pid))
-                trs.append(RemoteDMATransfer(dst_ids=ids, dma_engine_mask=m, remote_sem=S["%s%d" % (part, s)],
-                                             srcs=[view(s)], dsts=[view(s) for _ in ds]))
-                nsent += bin(m).count("1")
-            g.remote_dma_fused(trs, local_sem=S.sent)
+    for k, call in enumerate(calls[rank]):
+        if k == 2:
+            await_plane(g, owned[part[rank]][0])
+            lo, hi = grp[rank]
+            g.remote_dma_fused([transfer(T.ws[:, lo:hi], order[rank], "s", S["g%d" % rank])], local_sem=S.sent)
+            nsent += count(rank, order[rank], "s")
+        trs = []
+        for s, ds, kind in call:
+            if s not in waited:
+                waited.add(s)
+                await_slot(g, s, "q")
+            trs.append(transfer(codes(s), ds, kind, S["q%d" % s]))
+            nsent += count(rank, ds, kind)
+        g.remote_dma_fused(trs, local_sem=S.sent)
     g.wait_ge(S.sent, nsent)
 
     v, sc, te = g.vector, g.scalar, g.tensor
@@ -168,7 +203,7 @@ def rank_program(g, core, T, topo):
     for i in sorted(range(G), key=lambda i: mine[SLOT_A[i]][1]):
         a = SLOT_A[i]
         await_slot(te, a, "pq")
-        te.matmul_mx(T.ps[:, 512 * i:512 * i + NC], T.wc[:, a * NC:(a + 1) * NC], T.ws[:, a * NC:(a + 1) * NC],
+        te.matmul_mx(T.ps[:, 512 * i:512 * i + NC], T.wc[:, a * NC:(a + 1) * NC], plane(a),
                      T.xq[:, :], T.xs[:, :], True, True).then_inc(S["z%d" % i], 1)
     v.wait_ge(S.z0, 1)
     v.tensor_scalar(out=T.ht[:, 0:4 * NC:4], in0=T.ps[:, 0:NC], scalar1=0.0, scalar2=C,
@@ -191,7 +226,7 @@ def rank_program(g, core, T, topo):
             bank = (G + k) % 8
             out = T.ps[:, 512 * bank:512 * bank + NC]
             await_slot(te, s, "pq")
-            te.matmul_mx(out, T.wc[:, s * NC:(s + 1) * NC], T.ws[:, s * NC:(s + 1) * NC],
+            te.matmul_mx(out, T.wc[:, s * NC:(s + 1) * NC], plane(s),
                          T.hq[:, :], T.hs[:, :], True, True).then_inc(S["m%d" % k], 1)
             if k % 2 == 0:
                 v.wait_ge(S["m%d" % k], 1)

@@ -2,6 +2,7 @@ from concourse.bass import DstId, RemoteDMATransfer
 from concourse.mybir import dt, AluOpType, ActivationFunctionType
 
 N, NC, G = 8, 128, 2
+WORLD = 512
 C = 0.031
 SLOT_B = [0, 3] + [j + 2 for j in range(2, N)]
 SLOT_A = [1, 2]
@@ -19,8 +20,8 @@ SCRATCH = {
     "yt": ("sbuf", [128, N * NC], "float32"),
     "ps": ("psum", [128, 8 * 512], "float32"),
 }
-SEMAPHORES = (["lx", "sent", "xr", "z0", "z1", "hr", "hd", "st", "pl", "pc"]
-              + ["g%d" % r for r in range(N)] + ["q%d" % s for s in range(NSLOT)]
+SEMAPHORES = (["lx", "sent", "xr", "z0", "z1", "hr", "hd", "st"]
+              + ["p%d" % s for s in range(NSLOT)] + ["q%d" % s for s in range(NSLOT)]
               + ["m%d" % k for k in range(N)] + ["c%d" % k for k in range(N)])
 
 
@@ -35,10 +36,6 @@ def _part(m, kind):
 
 def _plan(cores, topo):
     n = len(cores)
-    lam = 1.0
-
-    def ok(a, b):
-        return topo.may_write(cores[a], cores[b])
 
     def rk(r):
         return topo.rack(topo.host(cores[r]))
@@ -50,159 +47,179 @@ def _plan(cores, topo):
         return topo.chip(cores[a]) == topo.chip(cores[b])
 
     mates = [[q for q in range(n) if topo.same_plane(cores[r], cores[q])] for r in range(n)]
-    part = [[q for q in range(n) if rk(q) != rk(r) and ok(r, q) and same_no(r, q)][0] for r in range(n)]
+    part = [[q for q in range(n) if rk(q) != rk(r) and topo.may_write(cores[r], cores[q]) and same_no(r, q)][0] for r in range(n)]
     order = [sorted(mates[r], key=lambda q: (same_host(r, q), not same_no(r, q))) for r in range(n)]
-    owner = {}
-    for j in range(N):
-        owner[SLOT_B[j]] = j
-    for i in range(G):
-        owner[SLOT_A[i]] = i
     owned = [SLOT_A[r:r + 1] + [SLOT_B[r]] for r in range(n)]
-    calls = [[] for _ in range(n)]
-    est = [dict() for _ in range(n)]
-    tq = [{"c": 0.0, "s": 0.0} for _ in range(n)]
+    helpers = []
+    for c in cores:
+        helpers.append([k for k in range(WORLD) if topo.host(k) == topo.host(c) and topo.chip(k) == topo.chip(c)
+                        and topo.die(k) != topo.die(c)][0])
 
-    def book(r, s, ds, kind, ready):
-        t = max(tq[r][kind], ready)
-        for d in ds:
-            t += 1.0
-            est[d][s] = t + lam
-        tq[r][kind] = t
+    def R(q):
+        return cores[q]
 
+    def H(q):
+        return helpers[q]
+
+    first = {c: [] for c in cores + helpers}
+    fwd = {c: [] for c in cores + helpers}
     for r in range(n):
-        for k, s in enumerate(owned[r]):
-            est[r][s] = 0.0
-            ds = order[r] if k == 0 else order[r][-1:] + order[r][:-1]
-            if k == 0:
-                calls[r].append([(s, ds, "s")])
-                calls[r].append([(s, [part[r]], "c")])
+        m1, m2, m3 = order[r]
+        p = part[r]
+        b = SLOT_B[r]
+        if len(owned[r]) > 1:
+            a = owned[r][0]
+            ds = [H(m2), R(m1), R(m3)]
+            first[R(r)].append([(("p", a), ds, "s"), (("p", a), [R(p)], "c")])
+            first[R(r)].append([(("p", b), [H(r)], "o")])
+            first[R(r)].append([(("q", a), ds, "s")])
+            first[R(r)].append([(("q", a), [R(p)], "c")])
+            first[R(r)].append([(("q", b), [R(p)], "c"), (("q", b), [R(m3), R(m1), R(m2)], "s")])
+            for k in ("p", "q"):
+                late = 1.0 if k == "q" else 0.0
+                fwd[R(m1)].append((2.0 + late, [((k, a), [R(part[m1])], "c")]))
+                fwd[H(m2)].append((1.0 + late, [((k, a), [R(part[m2])], "c"), ((k, a), [R(m2)], "o")]))
+                fwd[R(p)].append((2.0 + late, [((k, a), [R(part[m3])], "s")]))
+            fwd[R(p)].append((4.0, [(("q", b), [R(part[m1]), R(part[m2])], "s")]))
+            fwd[R(m3)].append((5.0, [(("q", b), [R(part[m3])], "c")]))
+        else:
+            first[R(r)].append([(("p", b), [H(r)], "o")])
+            first[R(r)].append([(("q", b), [R(q) for q in order[r]], "s")])
+            first[R(r)].append([(("q", b), [R(p)], "c")])
+            if len(owned[p]) > 1:
+                for i, m in enumerate(order[r]):
+                    fwd[R(m)].append((3.5 + i, [(("q", b), [R(part[m])], "c")]))
             else:
-                calls[r].append([(s, [part[r]], "c"), (s, ds, "s")])
-            book(r, s, [part[r]], "c", 0.0)
-            book(r, s, ds, "s", 0.0)
-    cf = [[] for _ in range(n)]
-    sf = [dict() for _ in range(n)]
-    for d in range(n):
-        todo = [s for s in SLOT_A + SLOT_B if rk(owner[s]) != rk(d) and owner[s] != part[d]]
-        for s in sorted(todo, key=lambda s: (s not in SLOT_A, not ok(owner[s], d), owner[s])):
-            o = owner[s]
-            if s in SLOT_A or len(owned[part[o]]) > 1:
-                cf[part[d]].append(s)
-            else:
-                sf[part[o]].setdefault(s, []).append(d)
-    for r in range(n):
-        items = [(est[r][s], 0, s, [part[r]], "c") for s in cf[r]]
-        items += [(est[r][s], 1, s, [q for q in order[r] if q in sf[r][s]], "s") for s in sf[r]]
-        for ready, _, s, ds, kind in sorted(items):
-            calls[r].append([(s, ds, kind)])
-            book(r, s, ds, kind, ready)
-    got = [{s: (owner[s] == d, est[d][s]) for s in est[d]} for d in range(n)]
-    return calls, got, part, order, owned
+                fwd[R(p)].append((3.6, [(("q", b), [R(q) for q in order[p]], "s")]))
+        first[H(r)].append([(("p", b), [R(q) for q in order[r]], "s"), (("p", b), [H(p), R(p)], "c")])
+        fwd[H(p)].append((3.0, [(("p", b), [R(q) for q in order[p]], "s")]))
+    prog = {c: first[c] + [call for _, call in sorted(fwd[c], key=lambda x: x[0])] for c in first}
+    return prog, owned
+
+
+def _expect(prog, cores, owned):
+    dur = {("q", "s"): 1.0, ("q", "c"): 1.6, ("q", "o"): 0.6, ("p", "s"): 0.3, ("p", "c"): 0.4, ("p", "o"): 0.2}
+    hop = 0.8
+    when = {c: {} for c in prog}
+    for r, c in enumerate(cores):
+        for s in owned[r]:
+            when[c][("q", s)] = 0.0
+            when[c][("p", s)] = 0.0
+    at = {c: 0 for c in prog}
+    tq = {c: hop for c in prog}
+    free = {}
+    moved = True
+    while moved:
+        moved = False
+        for c in prog:
+            while at[c] < len(prog[c]):
+                call = prog[c][at[c]]
+                if any(it not in when[c] for it, _, _ in call):
+                    break
+                tq[c] = max([tq[c]] + [when[c][it] + hop for it, _, _ in call])
+                for it, ds, fl in call:
+                    t = max(tq[c], free.get((c, fl), 0.0))
+                    for d in ds:
+                        t += dur[(it[0], fl)]
+                        when[d][it] = t
+                    free[(c, fl)] = t
+                at[c] += 1
+                moved = True
+    return when
 
 
 def rank_program(g, core, T, topo):
-    rank = T.rank_of(core)
-    if rank is None:
-        return
     cores = list(T.cores)
-    calls, got, part, order, owned = _plan(cores, topo)
+    prog, owned = _plan(cores, topo)
+    if core not in prog:
+        return
+    rank = T.rank_of(core)
     S = T.sem
-    mine = got[rank]
-
-    pos, span, grp = {}, {}, {}
-    for r in range(len(cores)):
-        if r < part[r]:
-            lo = len(pos)
-            for q in (r, part[r]):
-                a0 = len(pos)
-                for s in owned[q]:
-                    pos[s] = len(pos)
-                span[q] = (a0 * NC, len(pos) * NC)
-            grp[r] = grp[part[r]] = (lo * NC, len(pos) * NC)
 
     def codes(s):
         return T.wc[:, s * NC:(s + 1) * NC].bitcast(dt.uint8)
 
     def plane(s):
-        return T.ws[:, pos[s] * NC:(pos[s] + 1) * NC]
+        return T.ws[:, s * NC:(s + 1) * NC]
 
-    def engines(src, ds, kind):
+    def view(it):
+        return codes(it[1]) if it[0] == "q" else plane(it[1])
+
+    def sem(it):
+        return S["%s%d" % it]
+
+    def engines(src, ds, flow):
         m = -1
         for d in ds:
-            m &= topo.mask(cores[src], cores[d])
-        return _part(m, kind)
+            m &= topo.mask(src, d)
+        if flow == "o":
+            far = [c for c in cores if topo.same_plane(src, c)][0]
+            m &= ~topo.mask(src, far)
+        return _part(m, flow)
 
-    def count(src, ds, kind):
-        return bin(engines(src, ds, kind)).count("1")
+    def count(src, ds, flow):
+        return bin(engines(src, ds, flow)).count("1")
 
-    def transfer(view, ds, kind, sem):
+    def transfer(it, ds, flow):
         ids = []
         for d in ds:
-            rid, pid = topo.addr(cores[d], core)
+            rid, pid = topo.addr(d, core)
             ids.append(DstId(rid=rid, pnc=pid))
-        return RemoteDMATransfer(dst_ids=ids, dma_engine_mask=engines(rank, ds, kind), remote_sem=sem,
-                                 srcs=[view], dsts=[view for _ in ds])
+        return RemoteDMATransfer(dst_ids=ids, dma_engine_mask=engines(core, ds, flow), remote_sem=sem(it),
+                                 srcs=[view(it)], dsts=[view(it) for _ in ds])
 
-    if rank < G:
-        a = SLOT_A[rank]
-        g.scalar.dma_start(plane(a), T.az[:, :]).then_inc(S.pl, 16)
-        g.sync.dma_start(codes(a), T.ac[:, :]).then_inc(S["q%d" % a], 16)
-    b = SLOT_B[rank]
-    g.scalar.dma_start(plane(b), T.bs[:, :]).then_inc(S.pl, 16)
-    g.sync.dma_start(codes(b), T.bc[:, :]).then_inc(S["q%d" % b], 16)
-    g.scalar.dma_start(T.xt[:, :], T.x[:, :]).then_inc(S.lx, 16)
+    need = {}
+    if rank is not None:
+        for s in owned[rank]:
+            need[("q", s)] = 16
+            need[("p", s)] = 16
+    for c in prog:
+        for call in prog[c]:
+            for it, ds, fl in call:
+                if core in ds:
+                    need[it] = count(c, ds, fl)
 
-    need = {s: 16 for s in mine if mine[s][0]}
-    for r in range(len(cores)):
-        for call in calls[r]:
-            for s, ds, kind in call:
-                if rank in ds:
-                    need[s] = count(r, ds, kind)
-
-    def await_plane(q, s):
-        if s in owned[rank]:
-            q.wait_ge(S.pl, 16 * len(owned[rank]))
-        elif s in owned[part[rank]]:
-            q.wait_ge(S.pc, count(part[rank], [rank], "c"))
-        else:
-            m = [m for m in order[rank] if s in owned[m] or s in owned[part[m]]][0]
-            q.wait_ge(S["g%d" % m], count(m, order[m], "s"))
-
-    def await_slot(q, s, parts):
-        if "p" in parts:
-            await_plane(q, s)
-        if "q" in parts:
-            q.wait_ge(S["q%d" % s], need[s])
+    if rank is not None:
+        if rank < G:
+            a = SLOT_A[rank]
+            g.scalar.dma_start(plane(a), T.az[:, :]).then_inc(S["p%d" % a], 16)
+            g.sync.dma_start(codes(a), T.ac[:, :]).then_inc(S["q%d" % a], 16)
+        b = SLOT_B[rank]
+        g.scalar.dma_start(plane(b), T.bs[:, :]).then_inc(S["p%d" % b], 16)
+        g.sync.dma_start(codes(b), T.bc[:, :]).then_inc(S["q%d" % b], 16)
+        g.scalar.dma_start(T.xt[:, :], T.x[:, :]).then_inc(S.lx, 16)
 
     nsent = 0
-    await_plane(g, owned[rank][0])
-    lo, hi = span[rank]
-    g.remote_dma_fused([transfer(T.ws[:, lo:hi], [part[rank]], "c", S.pc)], local_sem=S.sent)
-    nsent += count(rank, [part[rank]], "c")
     waited = set()
-    for k, call in enumerate(calls[rank]):
-        if k == 2:
-            await_plane(g, owned[part[rank]][0])
-            lo, hi = grp[rank]
-            g.remote_dma_fused([transfer(T.ws[:, lo:hi], order[rank], "s", S["g%d" % rank])], local_sem=S.sent)
-            nsent += count(rank, order[rank], "s")
+    for call in prog[core]:
         trs = []
-        for s, ds, kind in call:
-            if s not in waited:
-                waited.add(s)
-                await_slot(g, s, "q")
-            trs.append(transfer(codes(s), ds, kind, S["q%d" % s]))
-            nsent += count(rank, ds, kind)
+        for it, ds, fl in call:
+            if it not in waited:
+                waited.add(it)
+                g.wait_ge(sem(it), need[it])
+            trs.append(transfer(it, ds, fl))
+            nsent += count(core, ds, fl)
         g.remote_dma_fused(trs, local_sem=S.sent)
     g.wait_ge(S.sent, nsent)
+    if rank is None:
+        return
+
+    mine = _expect(prog, cores, owned)[core]
+
+    def when(s):
+        return max(mine[("q", s)], mine[("p", s)])
+
+    def await_slot(q, s):
+        q.wait_ge(S["p%d" % s], need[("p", s)])
+        q.wait_ge(S["q%d" % s], need[("q", s)])
 
     v, sc, te = g.vector, g.scalar, g.tensor
     v.wait_ge(S.lx, 16)
     v.quantize_mx(T.xq[:, :], T.xs[:, :], T.xt[:, :]).then_inc(S.xr, 1)
     te.wait_ge(S.xr, 1)
-    for i in sorted(range(G), key=lambda i: mine[SLOT_A[i]][1]):
+    for i in sorted(range(G), key=lambda i: when(SLOT_A[i])):
         a = SLOT_A[i]
-        await_slot(te, a, "pq")
+        await_slot(te, a)
         te.matmul_mx(T.ps[:, 512 * i:512 * i + NC], T.wc[:, a * NC:(a + 1) * NC], plane(a),
                      T.xq[:, :], T.xs[:, :], True, True).then_inc(S["z%d" % i], 1)
     v.wait_ge(S.z0, 1)
@@ -218,14 +235,14 @@ def rank_program(g, core, T, topo):
     te.wait_ge(S.hd, 1)
 
     pairs = [[j for j in range(N) if topo.host(cores[j]) == h] for h in sorted({topo.host(c) for c in cores})]
-    pairs.sort(key=lambda p: (max(mine[SLOT_B[j]][1] for j in p), p[0]))
+    pairs.sort(key=lambda p: (max(when(SLOT_B[j]) for j in p), p[0]))
     k = 0
     for gi, p in enumerate(pairs):
-        for j in sorted(p, key=lambda j: mine[SLOT_B[j]][1]):
+        for j in sorted(p, key=lambda j: when(SLOT_B[j])):
             s = SLOT_B[j]
             bank = (G + k) % 8
             out = T.ps[:, 512 * bank:512 * bank + NC]
-            await_slot(te, s, "pq")
+            await_slot(te, s)
             te.matmul_mx(out, T.wc[:, s * NC:(s + 1) * NC], plane(s),
                          T.hq[:, :], T.hs[:, :], True, True).then_inc(S["m%d" % k], 1)
             if k % 2 == 0:

@@ -69,30 +69,42 @@ def _plan(cores, topo):
         b = SLOT_B[r]
         if len(owned[r]) > 1:
             a = owned[r][0]
-            ds = [H(m2), R(m1), R(m3)]
-            first[R(r)].append([(("p", a), ds, "s"), (("p", a), [R(p)], "c")])
-            first[R(r)].append([(("p", b), [H(r)], "o")])
-            first[R(r)].append([(("q", a), ds, "s")])
+            ds = [R(m1), H(m2), R(m3)]
+            first[R(r)].append([(("p", a), ds[:2], "s"), (("p", a), [R(p)], "c")])
+            first[R(r)].append([(("q", a), ds[:2], "s")])
             first[R(r)].append([(("q", a), [R(p)], "c")])
-            first[R(r)].append([(("q", b), [R(p)], "c"), (("q", b), [R(m3), R(m1), R(m2)], "s")])
+            first[R(r)].append([(("p", b), [H(r)], "o")])
+            first[R(r)].append([(("p", a), ds[2:], "s")])
+            first[R(r)].append([(("q", a), ds[2:], "s")])
+            first[R(r)].append([(("q", b), [R(p)], "c"), (("q", b), [R(m3), R(m1)], "s"), (("q", b), [H(r)], "o")])
+            fwd[H(r)].append((2.5, [(("q", b), [R(m2)], "s"), (("q", b), [R(part[m3])], "c")]))
             for k in ("p", "q"):
                 late = 1.0 if k == "q" else 0.0
                 fwd[R(m1)].append((2.0 + late, [((k, a), [R(part[m1])], "c")]))
                 fwd[H(m2)].append((1.0 + late, [((k, a), [R(part[m2])], "c"), ((k, a), [R(m2)], "o")]))
                 fwd[R(p)].append((2.0 + late, [((k, a), [R(part[m3])], "s")]))
             fwd[R(p)].append((4.0, [(("q", b), [R(part[m1]), R(part[m2])], "s")]))
-            fwd[R(m3)].append((5.0, [(("q", b), [R(part[m3])], "c")]))
         else:
             first[R(r)].append([(("p", b), [H(r)], "o")])
-            first[R(r)].append([(("q", b), [R(q) for q in order[r]], "s")])
-            first[R(r)].append([(("q", b), [R(p)], "c")])
+            first[R(r)].append([(("q", b), [R(m1), R(m2)], "s")])
+            first[R(r)].append([(("q", b), [R(p)], "c"), (("q", b), [H(r)], "o")])
             if len(owned[p]) > 1:
-                for i, m in enumerate(order[r]):
-                    fwd[R(m)].append((3.5 + i, [(("q", b), [R(part[m])], "c")]))
+                fwd[H(r)].append((2.5, [(("q", b), [R(m3)], "s"), (("q", b), [R(part[m3])], "c")]))
+                for i, m in enumerate((m1, m2)):
+                    fwd[R(m)].append((3.5 + 0.2 * i, [(("q", b), [R(part[m])], "c")]))
             else:
+                fwd[H(r)].append((2.5, [(("q", b), [R(m3)], "s")]))
                 fwd[R(p)].append((3.6, [(("q", b), [R(q) for q in order[p]], "s")]))
-        first[H(r)].append([(("p", b), [R(q) for q in order[r]], "s"), (("p", b), [H(p), R(p)], "c")])
-        fwd[H(p)].append((3.0, [(("p", b), [R(q) for q in order[p]], "s")]))
+    for r in range(n):
+        p = part[r]
+        b = SLOT_B[r]
+        tiles = sum(1 for call in first[R(r)] + [c for _, c in fwd[R(r)]] for it, _, fl in call if it[0] == "q" and fl == "c")
+        if len(owned[r]) == 1 and tiles <= 2:
+            first[H(r)].append([(("p", b), [R(q) for q in order[r]], "s")])
+            first[R(r)].append([(("p", b), [H(p)], "c")])
+        else:
+            first[H(r)].append([(("p", b), [R(q) for q in order[r]], "s"), (("p", b), [H(p)], "c")])
+        fwd[H(p)].append((3.0, [(("p", b), [R(q) for q in order[p]], "s"), (("p", b), [R(p)], "o")]))
     prog = {c: first[c] + [call for _, call in sorted(fwd[c], key=lambda x: x[0])] for c in first}
     return prog, owned
 

from concourse.bass import DstId, RemoteDMATransfer
from concourse.mybir import dt, AluOpType, ActivationFunctionType

N, NC, G = 8, 128, 2
WORLD = 512
C = 0.031
SLOT_B = [0, 3] + [j + 2 for j in range(2, N)]
SLOT_A = [1, 2]
NSLOT = N + G

SCRATCH = {
    "wc": ("sbuf", [128, NSLOT * NC], "float8_e4m3fn_x4"),
    "ws": ("sbuf", [128, NSLOT * NC], "uint8"),
    "xt": ("sbuf", [128, 4 * NC], "bfloat16"),
    "xq": ("sbuf", [128, NC], "float8_e4m3fn_x4"),
    "xs": ("sbuf", [128, NC], "uint8"),
    "ht": ("sbuf", [128, 4 * NC], "bfloat16"),
    "hq": ("sbuf", [128, NC], "float8_e4m3fn_x4"),
    "hs": ("sbuf", [128, NC], "uint8"),
    "yt": ("sbuf", [128, N * NC], "float32"),
    "ps": ("psum", [128, 8 * 512], "float32"),
}
SEMAPHORES = (["lx", "sent", "xr", "z0", "z1", "hr", "hd", "st"]
              + ["p%d" % s for s in range(NSLOT)] + ["q%d" % s for s in range(NSLOT)]
              + ["m%d" % k for k in range(N)] + ["c%d" % k for k in range(N)])


def _part(m, kind):
    bits = [b for b in range(32) if (m >> b) & 1]
    bits = bits[1::2] if kind == "c" else bits[0::2]
    out = 0
    for b in bits:
        out |= 1 << b
    return out


def _plan(cores, topo):
    n = len(cores)

    def rk(r):
        return topo.rack(topo.host(cores[r]))

    def same_host(a, b):
        return topo.host(cores[a]) == topo.host(cores[b])

    def same_no(a, b):
        return topo.chip(cores[a]) == topo.chip(cores[b])

    mates = [[q for q in range(n) if topo.same_plane(cores[r], cores[q])] for r in range(n)]
    part = [[q for q in range(n) if rk(q) != rk(r) and topo.may_write(cores[r], cores[q]) and same_no(r, q)][0] for r in range(n)]
    order = [sorted(mates[r], key=lambda q: (same_host(r, q), not same_no(r, q))) for r in range(n)]
    owned = [SLOT_A[r:r + 1] + [SLOT_B[r]] for r in range(n)]
    helpers = []
    for c in cores:
        helpers.append([k for k in range(WORLD) if topo.host(k) == topo.host(c) and topo.chip(k) == topo.chip(c)
                        and topo.die(k) != topo.die(c)][0])

    def R(q):
        return cores[q]

    def H(q):
        return helpers[q]

    first = {c: [] for c in cores + helpers}
    fwd = {c: [] for c in cores + helpers}
    for r in range(n):
        m1, m2, m3 = order[r]
        p = part[r]
        b = SLOT_B[r]
        if len(owned[r]) > 1:
            a = owned[r][0]
            ds = [R(m1), H(m2), R(m3)]
            first[R(r)].append([(("p", a), ds[:2], "s"), (("p", a), [R(p)], "c")])
            first[R(r)].append([(("q", a), ds[:2], "s")])
            first[R(r)].append([(("q", a), [R(p)], "c")])
            first[R(r)].append([(("p", b), [H(r)], "o")])
            first[R(r)].append([(("p", a), ds[2:], "s")])
            first[R(r)].append([(("q", a), ds[2:], "s")])
            first[R(r)].append([(("q", b), [R(p)], "c"), (("q", b), [R(m3), R(m1)], "s"), (("q", b), [H(r)], "o")])
            fwd[H(r)].append((2.5, [(("q", b), [R(m2)], "s"), (("q", b), [R(part[m3])], "c")]))
            for k in ("p", "q"):
                late = 1.0 if k == "q" else 0.0
                fwd[R(m1)].append((2.0 + late, [((k, a), [R(part[m1])], "c")]))
                fwd[H(m2)].append((1.0 + late, [((k, a), [R(part[m2])], "c"), ((k, a), [R(m2)], "o")]))
                fwd[R(p)].append((2.0 + late, [((k, a), [R(part[m3])], "s")]))
            fwd[R(p)].append((4.0, [(("q", b), [R(part[m1]), R(part[m2])], "s")]))
        else:
            first[R(r)].append([(("p", b), [H(r)], "o")])
            first[R(r)].append([(("q", b), [R(m1), R(m2)], "s")])
            first[R(r)].append([(("q", b), [R(p)], "c"), (("q", b), [H(r)], "o")])
            if len(owned[p]) > 1:
                fwd[H(r)].append((2.5, [(("q", b), [R(m3)], "s"), (("q", b), [R(part[m3])], "c")]))
                for i, m in enumerate((m1, m2)):
                    fwd[R(m)].append((3.5 + 0.2 * i, [(("q", b), [R(part[m])], "c")]))
            else:
                fwd[H(r)].append((2.5, [(("q", b), [R(m3)], "s")]))
                fwd[R(p)].append((3.6, [(("q", b), [R(q) for q in order[p]], "s")]))
    for r in range(n):
        p = part[r]
        b = SLOT_B[r]
        tiles = sum(1 for call in first[R(r)] + [c for _, c in fwd[R(r)]] for it, _, fl in call if it[0] == "q" and fl == "c")
        if len(owned[r]) == 1 and tiles <= 2:
            first[H(r)].append([(("p", b), [R(q) for q in order[r]], "s")])
            first[R(r)].append([(("p", b), [H(p)], "c")])
        else:
            first[H(r)].append([(("p", b), [R(q) for q in order[r]], "s"), (("p", b), [H(p)], "c")])
        fwd[H(p)].append((3.0, [(("p", b), [R(q) for q in order[p]], "s"), (("p", b), [R(p)], "o")]))
    prog = {c: first[c] + [call for _, call in sorted(fwd[c], key=lambda x: x[0])] for c in first}
    return prog, owned


def _expect(prog, cores, owned):
    dur = {("q", "s"): 1.0, ("q", "c"): 1.6, ("q", "o"): 0.6, ("p", "s"): 0.3, ("p", "c"): 0.4, ("p", "o"): 0.2}
    hop = 0.8
    when = {c: {} for c in prog}
    for r, c in enumerate(cores):
        for s in owned[r]:
            when[c][("q", s)] = 0.0
            when[c][("p", s)] = 0.0
    at = {c: 0 for c in prog}
    tq = {c: hop for c in prog}
    free = {}
    moved = True
    while moved:
        moved = False
        for c in prog:
            while at[c] < len(prog[c]):
                call = prog[c][at[c]]
                if any(it not in when[c] for it, _, _ in call):
                    break
                tq[c] = max([tq[c]] + [when[c][it] + hop for it, _, _ in call])
                for it, ds, fl in call:
                    t = max(tq[c], free.get((c, fl), 0.0))
                    for d in ds:
                        t += dur[(it[0], fl)]
                        when[d][it] = t
                    free[(c, fl)] = t
                at[c] += 1
                moved = True
    return when


def rank_program(g, core, T, topo):
    cores = list(T.cores)
    prog, owned = _plan(cores, topo)
    if core not in prog:
        return
    rank = T.rank_of(core)
    S = T.sem

    def codes(s):
        return T.wc[:, s * NC:(s + 1) * NC].bitcast(dt.uint8)

    def plane(s):
        return T.ws[:, s * NC:(s + 1) * NC]

    def view(it):
        return codes(it[1]) if it[0] == "q" else plane(it[1])

    def sem(it):
        return S["%s%d" % it]

    def engines(src, ds, flow):
        m = -1
        for d in ds:
            m &= topo.mask(src, d)
        if flow == "o":
            far = [c for c in cores if topo.same_plane(src, c)][0]
            m &= ~topo.mask(src, far)
        return _part(m, flow)

    def count(src, ds, flow):
        return bin(engines(src, ds, flow)).count("1")

    def transfer(it, ds, flow):
        ids = []
        for d in ds:
            rid, pid = topo.addr(d, core)
            ids.append(DstId(rid=rid, pnc=pid))
        return RemoteDMATransfer(dst_ids=ids, dma_engine_mask=engines(core, ds, flow), remote_sem=sem(it),
                                 srcs=[view(it)], dsts=[view(it) for _ in ds])

    need = {}
    if rank is not None:
        for s in owned[rank]:
            need[("q", s)] = 16
            need[("p", s)] = 16
    for c in prog:
        for call in prog[c]:
            for it, ds, fl in call:
                if core in ds:
                    need[it] = count(c, ds, fl)

    if rank is not None:
        if rank < G:
            a = SLOT_A[rank]
            g.scalar.dma_start(plane(a), T.az[:, :]).then_inc(S["p%d" % a], 16)
            g.sync.dma_start(codes(a), T.ac[:, :]).then_inc(S["q%d" % a], 16)
        b = SLOT_B[rank]
        g.scalar.dma_start(plane(b), T.bs[:, :]).then_inc(S["p%d" % b], 16)
        g.sync.dma_start(codes(b), T.bc[:, :]).then_inc(S["q%d" % b], 16)
        g.scalar.dma_start(T.xt[:, :], T.x[:, :]).then_inc(S.lx, 16)

    nsent = 0
    waited = set()
    for call in prog[core]:
        trs = []
        for it, ds, fl in call:
            if it not in waited:
                waited.add(it)
                g.wait_ge(sem(it), need[it])
            trs.append(transfer(it, ds, fl))
            nsent += count(core, ds, fl)
        g.remote_dma_fused(trs, local_sem=S.sent)
    g.wait_ge(S.sent, nsent)
    if rank is None:
        return

    mine = _expect(prog, cores, owned)[core]

    def when(s):
        return max(mine[("q", s)], mine[("p", s)])

    def await_slot(q, s):
        q.wait_ge(S["p%d" % s], need[("p", s)])
        q.wait_ge(S["q%d" % s], need[("q", s)])

    v, sc, te = g.vector, g.scalar, g.tensor
    v.wait_ge(S.lx, 16)
    v.quantize_mx(T.xq[:, :], T.xs[:, :], T.xt[:, :]).then_inc(S.xr, 1)
    te.wait_ge(S.xr, 1)
    for i in sorted(range(G), key=lambda i: when(SLOT_A[i])):
        a = SLOT_A[i]
        await_slot(te, a)
        te.matmul_mx(T.ps[:, 512 * i:512 * i + NC], T.wc[:, a * NC:(a + 1) * NC], plane(a),
                     T.xq[:, :], T.xs[:, :], True, True).then_inc(S["z%d" % i], 1)
    v.wait_ge(S.z0, 1)
    v.tensor_scalar(out=T.ht[:, 0:4 * NC:4], in0=T.ps[:, 0:NC], scalar1=0.0, scalar2=C,
                    op0=AluOpType.max, op1=AluOpType.mult).then_inc(S.hr, 1)
    v.tensor_scalar(out=T.ht[:, 1:4 * NC:4], in0=T.ps[:, 0:NC], scalar1=-C, scalar2=0.0,
                    op0=AluOpType.mult, op1=AluOpType.max).then_inc(S.hr, 1)
    sc.wait_ge(S.z1, 1)
    sc.activation(T.ht[:, 2:4 * NC:4], T.ps[:, 512:512 + NC], ActivationFunctionType.Relu, scale=C).then_inc(S.hr, 1)
    sc.activation(T.ht[:, 3:4 * NC:4], T.ps[:, 512:512 + NC], ActivationFunctionType.Relu, scale=-C).then_inc(S.hr, 1)
    v.wait_ge(S.hr, 4)
    v.quantize_mx(T.hq[:, :], T.hs[:, :], T.ht[:, :]).then_inc(S.hd, 1)
    te.wait_ge(S.hd, 1)

    pairs = [[j for j in range(N) if topo.host(cores[j]) == h] for h in sorted({topo.host(c) for c in cores})]
    pairs.sort(key=lambda p: (max(when(SLOT_B[j]) for j in p), p[0]))
    k = 0
    for gi, p in enumerate(pairs):
        for j in sorted(p, key=lambda j: when(SLOT_B[j])):
            s = SLOT_B[j]
            bank = (G + k) % 8
            out = T.ps[:, 512 * bank:512 * bank + NC]
            await_slot(te, s)
            te.matmul_mx(out, T.wc[:, s * NC:(s + 1) * NC], plane(s),
                         T.hq[:, :], T.hs[:, :], True, True).then_inc(S["m%d" % k], 1)
            if k % 2 == 0:
                v.wait_ge(S["m%d" % k], 1)
                v.tensor_copy(T.yt[:, j * NC:(j + 1) * NC], out).then_inc(S["c%d" % gi], 1)
            else:
                sc.wait_ge(S["m%d" % k], 1)
                sc.activation(T.yt[:, j * NC:(j + 1) * NC], out, ActivationFunctionType.Copy).then_inc(S["c%d" % gi], 1)
            k += 1
        lo, hi = min(p) * NC, (max(p) + 1) * NC
        g.sync.wait_ge(S["c%d" % gi], len(p))
        g.sync.dma_start(T.y[:, lo:hi], T.yt[:, lo:hi]).then_inc(S.st, 16)
    g.sync.wait_ge(S.st, 16 * len(pairs))
